import numpy as np
import ml_dtypes


def mxq(x, axis, fmt="e4m3"):
    dtype, down = {"e4m3": (ml_dtypes.float8_e4m3fn, 7), "e5m2": (ml_dtypes.float8_e5m2, 14)}[fmt]
    v = np.moveaxis(np.asarray(x, np.float32).astype(ml_dtypes.bfloat16).astype(np.float64), axis, -1)
    blocks = v.reshape(v.shape[:-1] + (-1, 32))
    amax = np.abs(blocks).max(-1, keepdims=True)
    byte = np.maximum(np.where(amax > 0, np.frexp(amax)[1] - 1 + 127, 0) - down, 1)
    scale = np.exp2(byte - 127.0)
    codes = (blocks / scale).astype(np.float32).astype(dtype).astype(np.float64)
    return np.moveaxis((codes * scale).reshape(v.shape), -1, axis)


WIDE = False


def mx_kscale(k):
    if not WIDE:
        return np.ones(k)
    levels = np.array([10, -10, 5, -5, 0])
    if k % 512:
        return np.exp2(np.random.permutation(np.resize(levels, k // 32))).repeat(32)
    a = np.empty((k // 512, 16))
    for p in range(k // 512):
        a[p, :8] = np.random.permutation(np.resize(levels, 8))
        for g in range(8):
            far = levels[np.abs(levels - a[p, g]) >= 10]
            a[p, g + 8] = far[np.random.randint(len(far))]
    return np.exp2(a.ravel()).repeat(32)


def f64(x):
    return np.asarray(x).astype(np.float64)


def striped(idx):
    return np.tile(idx.reshape(-1, 16).T, (8, 1)).astype(np.uint16)


def unstriped(offs):
    return offs[:16].T.reshape(-1).astype(np.int64)


def pack_weight(w):
    k, n = w.shape
    w = f64(np.asarray(w, np.float32).astype(ml_dtypes.bfloat16)).reshape(k // 32, 32, n)
    amax = np.abs(w).max(1)
    byte = np.clip(np.where(amax > 0, np.frexp(amax)[1] - 1 + 127 - 7, 1), 1, 254)
    scaled = (w * np.exp2(127.0 - byte)[:, None, :]).reshape(k, n).astype(np.float32)
    words = np.ascontiguousarray(scaled.reshape(k // 512, 128, 4, n).transpose(0, 1, 3, 2)).astype(ml_dtypes.float8_e4m3fn).view(np.uint8)
    return words, np.ascontiguousarray(byte.astype(np.uint8).reshape(k // 512, 16, n))


def unpack_weight(words, scales):
    g, p, n, _ = words.shape
    vals = np.ascontiguousarray(words).view(ml_dtypes.float8_e4m3fn).astype(np.float64) * np.repeat(np.exp2(scales.astype(np.float64) - 127.0), 8, axis=1)[..., None]
    return vals.transpose(0, 1, 3, 2).reshape(g * 512, n)


def silu(v):
    return v / (1.0 + np.exp(-np.maximum(v, -700.0)))


K, T, D, S, V, H, N = 512, 4096, 4, 1024, 256, 1024, 128


def setup_inputs():
    n = np.random.standard_normal
    s = mx_kscale(K)[:, None]
    u = mx_kscale(H)
    packed = pack_weight(n((K, T)) * s)
    return {
        "x_words": packed[0],
        "x_scales": packed[1],
        "w1": (n((K, H)) / np.sqrt(K) / s * u).astype(np.float32),
        "w2": (n((H, N)) / np.sqrt(H) / u[:, None]).astype(np.float32),
        "gate": np.tile(np.random.uniform(0.5, 1.5, V), (N, 1)).astype(np.float32),
        "offs": striped(np.random.permutation(T)[:S]),
        "pos1": striped(np.random.permutation(2 * V)[:V]),
    }


def reference(x_words, x_scales, w1, w2, gate, offs, pos1):
    h = silu(mxq(f64(w1), 0, "e4m3").T @ unpack_weight(x_words, x_scales)[:, unstriped(offs)])
    z = h.reshape(H, V, D).max(axis=2)
    out = np.zeros((N, 2 * V))
    out[:, unstriped(pos1)] = f64(gate) * (mxq(f64(w2), 0, "e4m3").T @ mxq(z, 0, "e4m3"))
    return out

@@ -1,0 +1,229 @@
+from contextlib import ExitStack
+
+import concourse.mybir as mybir
+
+K, T, D, S, V, H, N = 512, 4096, 4, 1024, 256, 1024, 128
+FLOPS = 2 * K * H * S + 2 * H * N * V
+
+F32 = mybir.dt.float32
+BF16 = mybir.dt.bfloat16
+I32 = mybir.dt.int32
+U32 = mybir.dt.uint32
+U16 = mybir.dt.uint16
+U8 = mybir.dt.uint8
+FP8X4 = mybir.dt.float8_e4m3fn_x4
+ACT = mybir.ActivationFunctionType
+ALU = mybir.AluOpType
+
+P = 128
+PACK = 4
+PASS = P * PACK
+BLOCKS = H // PASS
+HALVES = 2
+S_HALF = S // HALVES
+V_HALF = V // HALVES
+S_BANK = 128
+V_BANK = S_BANK // D
+BANKS = S_HALF // S_BANK
+
+
+def tile_picked_vpool_silu_p_kernel(
+    tc, x_words, x_scales, w1, w2, gate, offs, pos1, out
+):
+    nc = tc.nc
+    with ExitStack() as ctx:
+        keep = ctx.enter_context(tc.tile_pool(name="keep", bufs=1))
+        work = ctx.enter_context(tc.tile_pool(name="work", bufs=3))
+        psum1 = ctx.enter_context(tc.psum_pool(name="psum1", bufs=6))
+        psum2 = ctx.enter_context(tc.psum_pool(name="psum2", bufs=2))
+
+        offs_t = keep.tile([P, S // 16], U16, name="offs_t")
+        pos_t = keep.tile([P, V // 16], U16, name="pos_t")
+        xs = keep.tile([P, T], U8, name="xs", align_bytes=64)
+        xw = keep.tile([P, T], U32, name="xw", align_bytes=64)
+        plane = keep.tile([P, S], U8, name="plane", align_bytes=64)
+        gs = keep.tile([P, S], U8, name="gs", align_bytes=64)
+        frame = keep.tile([P, 2 * V], F32, name="frame")
+        warm = keep.tile([P, 1], F32, name="warm")
+        warm2 = keep.tile([P, 1], F32, name="warm2")
+
+        nc.vector.memset(xs[0:112, :].bitcast(I32), 0)
+        nc.vector.memset(plane[:].bitcast(I32), 0)
+        nc.gpsimd.memset(warm[:], 0.0)
+        nc.gpsimd.memset(frame[:], 0.0)
+
+        nc.sync.dma_start(offs_t[:], offs)
+        nc.sync.dma_start(out=xs[112:P, :].bitcast(I32), in_=x_scales[0].bitcast(I32))
+        nc.scalar.activation(warm2[:], warm[:], ACT.Silu)
+
+        nc.sync.dma_start(
+            out=xw[:].bitcast(I32), in_=x_words[0].rearrange("p c r -> p (c r)").bitcast(I32)
+        )
+        HC = PASS // 2
+        raw0 = []
+        for c in range(2):
+            raw = keep.tile([P, PACK, HC], F32, name="w1raw0%d" % c)
+            nc.sync.dma_start(out=raw[:], in_=w1[:, c * HC : (c + 1) * HC].rearrange("(p j) c -> p j c", j=PACK))
+            raw0.append(raw)
+        nc.sync.dma_start(pos_t[:], pos1)
+
+        nc.vector.tensor_copy(gs[:], xs[:].indirect(offs_t[:]))
+        for r in range(4):
+            nc.scalar.dma_start(
+                out=plane[32 * r : 32 * r + 4, :].bitcast(I32), in_=gs[112 + 4 * r : 116 + 4 * r, :].bitcast(I32)
+            )
+
+        raw1 = keep.tile([P, PACK, PASS], F32, name="w1raw1", tag="xs", align_bytes=64)
+        nc.sync.dma_start(out=raw1[:], in_=w1[:, PASS:].rearrange("(p j) c -> p j c", j=PACK))
+        late = keep.tile([P, BLOCKS * PACK * N + V], F32, name="late", align_bytes=64, tag="gs")
+        w2raw = late[:, 0 : BLOCKS * PACK * N]
+        gate_t = late[:, BLOCKS * PACK * N :]
+        nc.sync.dma_start(
+            out=w2raw.rearrange("p (b f) -> p b f", b=BLOCKS),
+            in_=w2.rearrange("(b p j) n -> p b (j n)", b=BLOCKS, j=PACK),
+        )
+        nc.sync.dma_start(out=gate_t, in_=gate)
+
+        gw = []
+        for hf in range(HALVES):
+            g = keep.tile([P, S_HALF], U32, name="gw%d" % hf, align_bytes=64)
+            cols = S_HALF // 16
+            nc.vector.tensor_copy(g[:], xw[:].indirect(offs_t[:, hf * cols : (hf + 1) * cols]))
+            gw.append(g)
+
+        def cast_w1(copy, grouped, m0, raw, r0, nm):
+            copy(
+                grouped[:].rearrange("p t m j -> p m j t")[:, m0 : m0 + nm],
+                raw[:].rearrange("p j (m t) -> p m j t", t=PACK)[:, r0 : r0 + nm],
+            )
+
+        def quant_w1(b, grouped, parts):
+            codes = keep.tile([P, PASS], U32, name="w1c%d" % b, align_bytes=64)
+            scales = keep.tile([P, PASS], U8, name="w1s%d" % b, align_bytes=64)
+            flat = grouped[:].rearrange("p t m j -> p (t m j)")
+            w = PASS // parts
+            for u in range(parts):
+                nc.vector.quantize_mx(
+                    out=codes[:, u * w : (u + 1) * w].bitcast(FP8X4),
+                    scales=scales[:, u * w : (u + 1) * w],
+                    in_=flat[:, u * w * PACK : (u + 1) * w * PACK],
+                )
+            return codes, scales
+
+        g0t = keep.tile([P, PACK, P, PACK], BF16, name="w1g0", align_bytes=64)
+        g1t = keep.tile([P, PACK, P, PACK], BF16, name="w1g1", align_bytes=64)
+        MV = 44
+        cast_w1(nc.scalar.copy, g0t, 0, raw0[0], 0, 64)
+        cast_w1(nc.vector.tensor_copy, g0t, 64, raw0[1], 0, MV)
+        cast_w1(nc.scalar.copy, g0t, 64 + MV, raw0[1], MV, 64 - MV)
+        w1q = [quant_w1(0, g0t, 4)]
+        cast_w1(nc.vector.tensor_copy, g1t, 0, raw1, 0, P)
+        w1q.append(quant_w1(1, g1t, 1))
+
+        zb = [keep.tile([P, V * PACK], BF16, name="z%d" % b, align_bytes=64) for b in range(BLOCKS)]
+        zc = [keep.tile([P, V], U32, name="zc%d" % b, align_bytes=64) for b in range(BLOCKS)]
+        zs = [keep.tile([P, V], U8, name="zs%d" % b, align_bytes=64) for b in range(BLOCKS)]
+
+        def silu_bank(h, hf, b, q, parts):
+            codes, scales = w1q[b]
+            acc = psum1.tile([P, PACK, S_BANK], F32, name="acc")
+            s0 = q * S_BANK
+            for t in range(PACK):
+                nc.tensor.matmul_mx(
+                    out=acc[:, t, :],
+                    lhsT=codes[:, t * P : (t + 1) * P].bitcast(FP8X4),
+                    lhsT_scale=scales[:, t * P : (t + 1) * P],
+                    rhs=gw[hf][:, s0 : s0 + S_BANK].bitcast(FP8X4),
+                    rhs_scale=plane[:, hf * S_HALF + s0 : hf * S_HALF + s0 + S_BANK],
+                    start=True,
+                    stop=True,
+                )
+            view = acc[:].rearrange("p t (v d) -> p d v t", d=D)
+            w = V_BANK // parts
+            for u in range(parts):
+                nc.scalar.activation(
+                    h[:, :, q * V_BANK + u * w : q * V_BANK + (u + 1) * w, :],
+                    view[:, :, u * w : (u + 1) * w, :],
+                    ACT.Silu,
+                )
+
+        def pool(h, hf, b, v0, nv):
+            m = work.tile([P, 2, nv * PACK], BF16, name="m")
+            hv = h[:].rearrange("p d v t -> p d (v t)")[:, :, v0 * PACK : (v0 + nv) * PACK]
+            nc.vector.tensor_tensor(m[:], hv[:, 0:2, :], hv[:, 2:4, :], ALU.max)
+            g0 = (hf * V_HALF + v0) * PACK
+            nc.vector.tensor_tensor(zb[b][:, g0 : g0 + nv * PACK], m[:, 0, :], m[:, 1, :], ALU.max)
+
+        def pool_reduce(h, hf, b, v0, nv):
+            hv = h[:].rearrange("p d v t -> p (v t) d")[:, v0 * PACK : (v0 + nv) * PACK, :]
+            g0 = (hf * V_HALF + v0) * PACK
+            nc.vector.tensor_reduce(zb[b][:, g0 : g0 + nv * PACK], hv, mybir.AxisListType.X, ALU.max)
+
+        def quant_z(b, g0, nv):
+            nc.vector.quantize_mx(
+                out=zc[b][:, g0 : g0 + nv].bitcast(FP8X4),
+                scales=zs[b][:, g0 : g0 + nv],
+                in_=zb[b][:, g0 * PACK : (g0 + nv) * PACK],
+            )
+
+        def layer1(hf, b):
+            h = work.tile([P, D, V_HALF, PACK], BF16, name="h")
+            for q in range(BANKS):
+                silu_bank(h, hf, b, q, 1)
+            pool(h, hf, b, 0, V_HALF)
+            quant_z(b, hf * V_HALF, V_HALF)
+
+        def layer2(g0, first, eng):
+            acc2 = psum2.tile([P, V_HALF], F32, name="acc2")
+            for b in range(BLOCKS):
+                nc.tensor.matmul_mx(
+                    out=acc2[:],
+                    lhsT=w2c[:, b * N : (b + 1) * N].bitcast(FP8X4),
+                    lhsT_scale=w2s[:, b * N : (b + 1) * N],
+                    rhs=zc[b][:, g0 : g0 + V_HALF].bitcast(FP8X4),
+                    rhs_scale=zs[b][:, g0 : g0 + V_HALF],
+                    start=(b == 0),
+                    stop=(b == BLOCKS - 1),
+                )
+            nv = g0 + V_HALF - first
+            y = work.tile([P, nv], F32, name="y")
+            if eng == "s":
+                nc.scalar.copy(y[:], acc2[:, first - g0 :])
+            else:
+                nc.vector.tensor_copy(y[:], acc2[:, first - g0 :])
+            nc.vector.tensor_tensor(
+                frame[:].indirect(pos_t[:, first // 16 : (first + nv) // 16]),
+                y[:],
+                gate_t[:, first : first + nv],
+                ALU.mult,
+            )
+
+        layer1(0, 0)
+
+        w2g = keep.tile([P, BLOCKS, N, PACK], BF16, name="w2g", align_bytes=64)
+        nc.vector.tensor_copy(
+            out=w2g[:].rearrange("p b (c i) j -> p b c j i", i=4),
+            in_=w2raw.rearrange("p (b j c i) -> p b c j i", b=BLOCKS, j=PACK, i=4),
+        )
+        w2c = keep.tile([P, BLOCKS * N], U32, name="w2c", align_bytes=64)
+        w2s = keep.tile([P, BLOCKS * N], U8, name="w2s", align_bytes=64)
+        nc.vector.quantize_mx(
+            out=w2c[:].bitcast(FP8X4), scales=w2s[:], in_=w2g[:].rearrange("p b n j -> p (b n j)")
+        )
+        layer1(1, 0)
+        layer1(0, 1)
+        layer2(0, 0, "s")
+        h = work.tile([P, D, V_HALF, PACK], BF16, name="h")
+        silu_bank(h, 1, 1, 0, 1)
+        silu_bank(h, 1, 1, 1, 1)
+        pool(h, 1, 1, 0, 64)
+        quant_z(1, 128, 64)
+        layer2(64, 128, "v")
+        silu_bank(h, 1, 1, 2, 1)
+        pool(h, 1, 1, 64, 32)
+        silu_bank(h, 1, 1, 3, 2)
+        pool_reduce(h, 1, 1, 96, 16)
+        pool_reduce(h, 1, 1, 112, 16)
+        quant_z(1, 192, 64)
+        layer2(128, 192, "s")
+        nc.sync.dma_start(out=out, in_=frame[:])

@@ -53,7 +53,7 @@ def tile_picked_vpool_silu_p_kernel(
         nc.gpsimd.memset(frame[:], 0.0)
 
         nc.sync.dma_start(offs_t[:], offs)
-        nc.sync.dma_start(out=xs[112:P, :].bitcast(I32), in_=x_scales[0].bitcast(I32))
+        nc.scalar.dma_start(out=xs[112:P, :].bitcast(I32), in_=x_scales[0].bitcast(I32))
         nc.scalar.activation(warm2[:], warm[:], ACT.Silu)
 
         nc.sync.dma_start(
@@ -62,9 +62,9 @@ def tile_picked_vpool_silu_p_kernel(
         HC = PASS // 2
         raw0 = []
         for c in range(2):
-            raw = keep.tile([P, PACK, HC], F32, name="w1raw0%d" % c)
+            raw = keep.tile([P, PACK, HC], F32, name="w1raw0%d" % c, align_bytes=64)
             nc.sync.dma_start(out=raw[:], in_=w1[:, c * HC : (c + 1) * HC].rearrange("(p j) c -> p j c", j=PACK))
-            raw0.append(raw)
+            raw0.append(raw[:])
         nc.sync.dma_start(pos_t[:], pos1)
 
         nc.vector.tensor_copy(gs[:], xs[:].indirect(offs_t[:]))
@@ -73,9 +73,13 @@ def tile_picked_vpool_silu_p_kernel(
                 out=plane[32 * r : 32 * r + 4, :].bitcast(I32), in_=gs[112 + 4 * r : 116 + 4 * r, :].bitcast(I32)
             )
 
-        raw1 = keep.tile([P, PACK, PASS], F32, name="w1raw1", tag="xs", align_bytes=64)
-        nc.sync.dma_start(out=raw1[:], in_=w1[:, PASS:].rearrange("(p j) c -> p j c", j=PACK))
-        late = keep.tile([P, BLOCKS * PACK * N + V], F32, name="late", align_bytes=64, tag="gs")
+        raw1 = keep.tile([P, 2 * PACK * HC], F32, name="w1raw1", tag="xs", align_bytes=64)
+        raw1c = [raw1[:, c * PACK * HC : (c + 1) * PACK * HC].rearrange("p (j c) -> p j c", j=PACK) for c in range(2)]
+        for c in range(2):
+            nc.sync.dma_start(
+                out=raw1c[c], in_=w1[:, PASS + c * HC : PASS + (c + 1) * HC].rearrange("(p j) c -> p j c", j=PACK)
+            )
+        late = keep.tile([P, BLOCKS * PACK * N + V], F32, name="late", align_bytes=64, tag="w1raw00")
         w2raw = late[:, 0 : BLOCKS * PACK * N]
         gate_t = late[:, BLOCKS * PACK * N :]
         nc.sync.dma_start(
@@ -84,17 +88,30 @@ def tile_picked_vpool_silu_p_kernel(
         )
         nc.sync.dma_start(out=gate_t, in_=gate)
 
-        gw = []
-        for hf in range(HALVES):
-            g = keep.tile([P, S_HALF], U32, name="gw%d" % hf, align_bytes=64)
+        def gather_words(hf, tag):
+            g = keep.tile([P, S_HALF], U32, name="gw%d" % hf, align_bytes=64, tag=tag)
             cols = S_HALF // 16
             nc.vector.tensor_copy(g[:], xw[:].indirect(offs_t[:, hf * cols : (hf + 1) * cols]))
-            gw.append(g)
+            return g
+
+        gw = [gather_words(0, "gw0")]
+
+        for u in range(3):
+            wacc = psum2.tile([P, S_HALF], F32, name="acc2")
+            nc.tensor.matmul_mx(
+                out=wacc[:],
+                lhsT=gw[0][:, 0:P].bitcast(FP8X4),
+                lhsT_scale=gs[:, 0:P],
+                rhs=gw[0][:].bitcast(FP8X4),
+                rhs_scale=gs[:, 0:S_HALF],
+                start=True,
+                stop=True,
+            )
 
         def cast_w1(copy, grouped, m0, raw, r0, nm):
             copy(
-                grouped[:].rearrange("p t m j -> p m j t")[:, m0 : m0 + nm],
-                raw[:].rearrange("p j (m t) -> p m j t", t=PACK)[:, r0 : r0 + nm],
+                grouped[:].rearrange("p (u e) m j -> p u m j e", e=2)[:, :, m0 : m0 + nm],
+                raw.rearrange("p j (m u e) -> p u m j e", u=2, e=2)[:, :, r0 : r0 + nm],
             )
 
         def quant_w1(b, grouped, parts):
@@ -113,20 +130,32 @@ def tile_picked_vpool_silu_p_kernel(
         g0t = keep.tile([P, PACK, P, PACK], BF16, name="w1g0", align_bytes=64)
         g1t = keep.tile([P, PACK, P, PACK], BF16, name="w1g1", align_bytes=64)
         MV = 44
-        cast_w1(nc.scalar.copy, g0t, 0, raw0[0], 0, 64)
-        cast_w1(nc.vector.tensor_copy, g0t, 64, raw0[1], 0, MV)
-        cast_w1(nc.scalar.copy, g0t, 64 + MV, raw0[1], MV, 64 - MV)
-        w1q = [quant_w1(0, g0t, 4)]
-        cast_w1(nc.vector.tensor_copy, g1t, 0, raw1, 0, P)
+        codes0 = keep.tile([P, PASS], U32, name="w1c0", align_bytes=64)
+        scales0 = keep.tile([P, PASS], U8, name="w1s0", align_bytes=64)
+        for c in range(2):
+            cast_w1(nc.vector.tensor_copy, g0t, c * 64, raw0[c], 0, MV)
+            cast_w1(nc.scalar.copy, g0t, c * 64 + MV, raw0[c], MV, 64 - MV)
+            for t in range(PACK):
+                m0 = t * P + c * 64
+                nc.vector.quantize_mx(
+                    out=codes0[:, m0 : m0 + 64].bitcast(FP8X4),
+                    scales=scales0[:, m0 : m0 + 64],
+                    in_=g0t[:, t, c * 64 : (c + 1) * 64, :].rearrange("p m j -> p (m j)"),
+                )
+        w1q = [(codes0, scales0)]
+        gw.append(gather_words(1, "w1g0"))
+        for c in range(2):
+            cast_w1(nc.vector.tensor_copy, g1t, c * 64, raw1c[c], 0, 64)
         w1q.append(quant_w1(1, g1t, 1))
 
         zb = [keep.tile([P, V * PACK], BF16, name="z%d" % b, align_bytes=64) for b in range(BLOCKS)]
         zc = [keep.tile([P, V], U32, name="zc%d" % b, align_bytes=64) for b in range(BLOCKS)]
         zs = [keep.tile([P, V], U8, name="zs%d" % b, align_bytes=64) for b in range(BLOCKS)]
 
-        def silu_bank(h, hf, b, q, parts):
+        def silu_bank(h, slot, b, bank, parts):
             codes, scales = w1q[b]
             acc = psum1.tile([P, PACK, S_BANK], F32, name="acc")
+            hf, q = divmod(bank, BANKS)
             s0 = q * S_BANK
             for t in range(PACK):
                 nc.tensor.matmul_mx(
@@ -134,7 +163,7 @@ def tile_picked_vpool_silu_p_kernel(
                     lhsT=codes[:, t * P : (t + 1) * P].bitcast(FP8X4),
                     lhsT_scale=scales[:, t * P : (t + 1) * P],
                     rhs=gw[hf][:, s0 : s0 + S_BANK].bitcast(FP8X4),
-                    rhs_scale=plane[:, hf * S_HALF + s0 : hf * S_HALF + s0 + S_BANK],
+                    rhs_scale=plane[:, bank * S_BANK : (bank + 1) * S_BANK],
                     start=True,
                     stop=True,
                 )
@@ -142,22 +171,23 @@ def tile_picked_vpool_silu_p_kernel(
             w = V_BANK // parts
             for u in range(parts):
                 nc.scalar.activation(
-                    h[:, :, q * V_BANK + u * w : q * V_BANK + (u + 1) * w, :],
+                    h[:, :, slot * V_BANK + u * w : slot * V_BANK + (u + 1) * w, :],
                     view[:, :, u * w : (u + 1) * w, :],
                     ACT.Silu,
                 )
 
-        def pool(h, hf, b, v0, nv):
-            m = work.tile([P, 2, nv * PACK], BF16, name="m")
+        def pool(h, b, v0, nv, g0, tag=None):
+            if tag:
+                m = keep.tile([P, 2, nv * PACK], BF16, name="m" + tag, tag=tag, align_bytes=64)
+            else:
+                m = work.tile([P, 2, nv * PACK], BF16, name="m")
             hv = h[:].rearrange("p d v t -> p d (v t)")[:, :, v0 * PACK : (v0 + nv) * PACK]
             nc.vector.tensor_tensor(m[:], hv[:, 0:2, :], hv[:, 2:4, :], ALU.max)
-            g0 = (hf * V_HALF + v0) * PACK
-            nc.vector.tensor_tensor(zb[b][:, g0 : g0 + nv * PACK], m[:, 0, :], m[:, 1, :], ALU.max)
+            nc.vector.tensor_tensor(zb[b][:, g0 * PACK : (g0 + nv) * PACK], m[:, 0, :], m[:, 1, :], ALU.max)
 
-        def pool_reduce(h, hf, b, v0, nv):
+        def pool_reduce(h, b, v0, nv, g0):
             hv = h[:].rearrange("p d v t -> p (v t) d")[:, v0 * PACK : (v0 + nv) * PACK, :]
-            g0 = (hf * V_HALF + v0) * PACK
-            nc.vector.tensor_reduce(zb[b][:, g0 : g0 + nv * PACK], hv, mybir.AxisListType.X, ALU.max)
+            nc.vector.tensor_reduce(zb[b][:, g0 * PACK : (g0 + nv) * PACK], hv, mybir.AxisListType.X, ALU.max)
 
         def quant_z(b, g0, nv):
             nc.vector.quantize_mx(
@@ -166,14 +196,16 @@ def tile_picked_vpool_silu_p_kernel(
                 in_=zb[b][:, g0 * PACK : (g0 + nv) * PACK],
             )
 
-        def layer1(hf, b):
-            h = work.tile([P, D, V_HALF, PACK], BF16, name="h")
-            for q in range(BANKS):
-                silu_bank(h, hf, b, q, 1)
-            pool(h, hf, b, 0, V_HALF)
-            quant_z(b, hf * V_HALF, V_HALF)
+        def layer1(b, bank0, nb, quant=True, tag=None):
+            h = work.tile([P, D, nb * V_BANK, PACK], BF16, name="h")
+            for q in range(nb):
+                silu_bank(h, q, b, bank0 + q, 1)
+            pool(h, b, 0, nb * V_BANK, bank0 * V_BANK, tag)
+            if quant:
+                quant_z(b, bank0 * V_BANK, nb * V_BANK)
+            return h
 
-        def layer2(g0, first, eng):
+        def layer2(g0, first, eng, tag=None):
             acc2 = psum2.tile([P, V_HALF], F32, name="acc2")
             for b in range(BLOCKS):
                 nc.tensor.matmul_mx(
@@ -186,7 +218,10 @@ def tile_picked_vpool_silu_p_kernel(
                     stop=(b == BLOCKS - 1),
                 )
             nv = g0 + V_HALF - first
-            y = work.tile([P, nv], F32, name="y")
+            if tag:
+                y = keep.tile([P, nv], F32, name="y" + tag, tag=tag, align_bytes=64)
+            else:
+                y = work.tile([P, nv], F32, name="y")
             if eng == "s":
                 nc.scalar.copy(y[:], acc2[:, first - g0 :])
             else:
@@ -198,32 +233,28 @@ def tile_picked_vpool_silu_p_kernel(
                 ALU.mult,
             )
 
-        layer1(0, 0)
-
+        layer1(0, 0, 4, tag="w1g1")
         w2g = keep.tile([P, BLOCKS, N, PACK], BF16, name="w2g", align_bytes=64)
-        nc.vector.tensor_copy(
-            out=w2g[:].rearrange("p b (c i) j -> p b c j i", i=4),
-            in_=w2raw.rearrange("p (b j c i) -> p b c j i", b=BLOCKS, j=PACK, i=4),
-        )
+        for b, copy in enumerate((nc.vector.tensor_copy, nc.vector.tensor_copy)):
+            copy(
+                w2g[:, b].rearrange("p (c i) j -> p c j i", i=4),
+                w2raw[:, b * PACK * N : (b + 1) * PACK * N].rearrange("p (j c i) -> p c j i", j=PACK, i=4),
+            )
         w2c = keep.tile([P, BLOCKS * N], U32, name="w2c", align_bytes=64)
         w2s = keep.tile([P, BLOCKS * N], U8, name="w2s", align_bytes=64)
         nc.vector.quantize_mx(
             out=w2c[:].bitcast(FP8X4), scales=w2s[:], in_=w2g[:].rearrange("p b n j -> p (b n j)")
         )
-        layer1(1, 0)
-        layer1(0, 1)
+        layer1(0, 4, 3, quant=False)
+        quant_z(0, 128, 64)
+        layer1(1, 0, 4)
         layer2(0, 0, "s")
-        h = work.tile([P, D, V_HALF, PACK], BF16, name="h")
-        silu_bank(h, 1, 1, 0, 1)
-        silu_bank(h, 1, 1, 1, 1)
-        pool(h, 1, 1, 0, 64)
-        quant_z(1, 128, 64)
-        layer2(64, 128, "v")
-        silu_bank(h, 1, 1, 2, 1)
-        pool(h, 1, 1, 64, 32)
-        silu_bank(h, 1, 1, 3, 2)
-        pool_reduce(h, 1, 1, 96, 16)
-        pool_reduce(h, 1, 1, 112, 16)
+        layer1(0, 7, 1, quant=False)
+        quant_z(0, 192, 64)
+        layer1(1, 4, 2)
+        layer1(1, 6, 1, quant=False)
+        h = layer1(1, 7, 1, quant=False, tag="last")
         quant_z(1, 192, 64)
+        layer2(64, 128, "s", tag="last")
         layer2(128, 192, "s")
         nc.sync.dma_start(out=out, in_=frame[:])

from contextlib import ExitStack

import concourse.mybir as mybir

K, T, D, S, V, H, N = 512, 4096, 4, 1024, 256, 1024, 128
FLOPS = 2 * K * H * S + 2 * H * N * V

F32 = mybir.dt.float32
BF16 = mybir.dt.bfloat16
I32 = mybir.dt.int32
U32 = mybir.dt.uint32
U16 = mybir.dt.uint16
U8 = mybir.dt.uint8
FP8X4 = mybir.dt.float8_e4m3fn_x4
ACT = mybir.ActivationFunctionType
ALU = mybir.AluOpType

P = 128
PACK = 4
PASS = P * PACK
BLOCKS = H // PASS
HALVES = 2
S_HALF = S // HALVES
V_HALF = V // HALVES
S_BANK = 128
V_BANK = S_BANK // D
BANKS = S_HALF // S_BANK


def tile_picked_vpool_silu_p_kernel(
    tc, x_words, x_scales, w1, w2, gate, offs, pos1, out
):
    nc = tc.nc
    with ExitStack() as ctx:
        keep = ctx.enter_context(tc.tile_pool(name="keep", bufs=1))
        work = ctx.enter_context(tc.tile_pool(name="work", bufs=3))
        psum1 = ctx.enter_context(tc.psum_pool(name="psum1", bufs=6))
        psum2 = ctx.enter_context(tc.psum_pool(name="psum2", bufs=2))

        offs_t = keep.tile([P, S // 16], U16, name="offs_t")
        pos_t = keep.tile([P, V // 16], U16, name="pos_t")
        xs = keep.tile([P, T], U8, name="xs", align_bytes=64)
        xw = keep.tile([P, T], U32, name="xw", align_bytes=64)
        plane = keep.tile([P, S], U8, name="plane", align_bytes=64)
        gs = keep.tile([P, S], U8, name="gs", align_bytes=64)
        frame = keep.tile([P, 2 * V], F32, name="frame")
        warm = keep.tile([P, 1], F32, name="warm")
        warm2 = keep.tile([P, 1], F32, name="warm2")

        nc.vector.memset(xs[0:112, :].bitcast(I32), 0)
        nc.vector.memset(plane[:].bitcast(I32), 0)
        nc.gpsimd.memset(warm[:], 0.0)
        nc.gpsimd.memset(frame[:], 0.0)

        nc.sync.dma_start(offs_t[:], offs)
        nc.scalar.dma_start(out=xs[112:P, :].bitcast(I32), in_=x_scales[0].bitcast(I32))
        nc.scalar.activation(warm2[:], warm[:], ACT.Silu)

        nc.sync.dma_start(
            out=xw[:].bitcast(I32), in_=x_words[0].rearrange("p c r -> p (c r)").bitcast(I32)
        )
        HC = PASS // 2
        raw0 = []
        for c in range(2):
            raw = keep.tile([P, PACK, HC], F32, name="w1raw0%d" % c, align_bytes=64)
            nc.sync.dma_start(out=raw[:], in_=w1[:, c * HC : (c + 1) * HC].rearrange("(p j) c -> p j c", j=PACK))
            raw0.append(raw[:])
        nc.sync.dma_start(pos_t[:], pos1)

        nc.vector.tensor_copy(gs[:], xs[:].indirect(offs_t[:]))
        for r in range(4):
            nc.scalar.dma_start(
                out=plane[32 * r : 32 * r + 4, :].bitcast(I32), in_=gs[112 + 4 * r : 116 + 4 * r, :].bitcast(I32)
            )

        raw1 = keep.tile([P, 2 * PACK * HC], F32, name="w1raw1", tag="xs", align_bytes=64)
        raw1c = [raw1[:, c * PACK * HC : (c + 1) * PACK * HC].rearrange("p (j c) -> p j c", j=PACK) for c in range(2)]
        for c in range(2):
            nc.sync.dma_start(
                out=raw1c[c], in_=w1[:, PASS + c * HC : PASS + (c + 1) * HC].rearrange("(p j) c -> p j c", j=PACK)
            )
        late = keep.tile([P, BLOCKS * PACK * N + V], F32, name="late", align_bytes=64, tag="w1raw00")
        w2raw = late[:, 0 : BLOCKS * PACK * N]
        gate_t = late[:, BLOCKS * PACK * N :]
        nc.sync.dma_start(
            out=w2raw.rearrange("p (b f) -> p b f", b=BLOCKS),
            in_=w2.rearrange("(b p j) n -> p b (j n)", b=BLOCKS, j=PACK),
        )
        nc.sync.dma_start(out=gate_t, in_=gate)

        def gather_words(hf, tag):
            g = keep.tile([P, S_HALF], U32, name="gw%d" % hf, align_bytes=64, tag=tag)
            cols = S_HALF // 16
            nc.vector.tensor_copy(g[:], xw[:].indirect(offs_t[:, hf * cols : (hf + 1) * cols]))
            return g

        gw = [gather_words(0, "gw0")]

        for u in range(3):
            wacc = psum2.tile([P, S_HALF], F32, name="acc2")
            nc.tensor.matmul_mx(
                out=wacc[:],
                lhsT=gw[0][:, 0:P].bitcast(FP8X4),
                lhsT_scale=gs[:, 0:P],
                rhs=gw[0][:].bitcast(FP8X4),
                rhs_scale=gs[:, 0:S_HALF],
                start=True,
                stop=True,
            )

        def cast_w1(copy, grouped, m0, raw, r0, nm):
            copy(
                grouped[:].rearrange("p (u e) m j -> p u m j e", e=2)[:, :, m0 : m0 + nm],
                raw.rearrange("p j (m u e) -> p u m j e", u=2, e=2)[:, :, r0 : r0 + nm],
            )

        def quant_w1(b, grouped, parts):
            codes = keep.tile([P, PASS], U32, name="w1c%d" % b, align_bytes=64)
            scales = keep.tile([P, PASS], U8, name="w1s%d" % b, align_bytes=64)
            flat = grouped[:].rearrange("p t m j -> p (t m j)")
            w = PASS // parts
            for u in range(parts):
                nc.vector.quantize_mx(
                    out=codes[:, u * w : (u + 1) * w].bitcast(FP8X4),
                    scales=scales[:, u * w : (u + 1) * w],
                    in_=flat[:, u * w * PACK : (u + 1) * w * PACK],
                )
            return codes, scales

        g0t = keep.tile([P, PACK, P, PACK], BF16, name="w1g0", align_bytes=64)
        g1t = keep.tile([P, PACK, P, PACK], BF16, name="w1g1", align_bytes=64)
        MV = 44
        codes0 = keep.tile([P, PASS], U32, name="w1c0", align_bytes=64)
        scales0 = keep.tile([P, PASS], U8, name="w1s0", align_bytes=64)
        for c in range(2):
            cast_w1(nc.vector.tensor_copy, g0t, c * 64, raw0[c], 0, MV)
            cast_w1(nc.scalar.copy, g0t, c * 64 + MV, raw0[c], MV, 64 - MV)
            for t in range(PACK):
                m0 = t * P + c * 64
                nc.vector.quantize_mx(
                    out=codes0[:, m0 : m0 + 64].bitcast(FP8X4),
                    scales=scales0[:, m0 : m0 + 64],
                    in_=g0t[:, t, c * 64 : (c + 1) * 64, :].rearrange("p m j -> p (m j)"),
                )
        w1q = [(codes0, scales0)]
        gw.append(gather_words(1, "w1g0"))
        for c in range(2):
            cast_w1(nc.vector.tensor_copy, g1t, c * 64, raw1c[c], 0, 64)
        w1q.append(quant_w1(1, g1t, 1))

        zb = [keep.tile([P, V * PACK], BF16, name="z%d" % b, align_bytes=64) for b in range(BLOCKS)]
        zc = [keep.tile([P, V], U32, name="zc%d" % b, align_bytes=64) for b in range(BLOCKS)]
        zs = [keep.tile([P, V], U8, name="zs%d" % b, align_bytes=64) for b in range(BLOCKS)]

        def silu_bank(h, slot, b, bank, parts):
            codes, scales = w1q[b]
            acc = psum1.tile([P, PACK, S_BANK], F32, name="acc")
            hf, q = divmod(bank, BANKS)
            s0 = q * S_BANK
            for t in range(PACK):
                nc.tensor.matmul_mx(
                    out=acc[:, t, :],
                    lhsT=codes[:, t * P : (t + 1) * P].bitcast(FP8X4),
                    lhsT_scale=scales[:, t * P : (t + 1) * P],
                    rhs=gw[hf][:, s0 : s0 + S_BANK].bitcast(FP8X4),
                    rhs_scale=plane[:, bank * S_BANK : (bank + 1) * S_BANK],
                    start=True,
                    stop=True,
                )
            view = acc[:].rearrange("p t (v d) -> p d v t", d=D)
            w = V_BANK // parts
            for u in range(parts):
                nc.scalar.activation(
                    h[:, :, slot * V_BANK + u * w : slot * V_BANK + (u + 1) * w, :],
                    view[:, :, u * w : (u + 1) * w, :],
                    ACT.Silu,
                )

        def pool(h, b, v0, nv, g0, tag=None):
            if tag:
                m = keep.tile([P, 2, nv * PACK], BF16, name="m" + tag, tag=tag, align_bytes=64)
            else:
                m = work.tile([P, 2, nv * PACK], BF16, name="m")
            hv = h[:].rearrange("p d v t -> p d (v t)")[:, :, v0 * PACK : (v0 + nv) * PACK]
            nc.vector.tensor_tensor(m[:], hv[:, 0:2, :], hv[:, 2:4, :], ALU.max)
            nc.vector.tensor_tensor(zb[b][:, g0 * PACK : (g0 + nv) * PACK], m[:, 0, :], m[:, 1, :], ALU.max)

        def pool_reduce(h, b, v0, nv, g0):
            hv = h[:].rearrange("p d v t -> p (v t) d")[:, v0 * PACK : (v0 + nv) * PACK, :]
            nc.vector.tensor_reduce(zb[b][:, g0 * PACK : (g0 + nv) * PACK], hv, mybir.AxisListType.X, ALU.max)

        def quant_z(b, g0, nv):
            nc.vector.quantize_mx(
                out=zc[b][:, g0 : g0 + nv].bitcast(FP8X4),
                scales=zs[b][:, g0 : g0 + nv],
                in_=zb[b][:, g0 * PACK : (g0 + nv) * PACK],
            )

        def layer1(b, bank0, nb, quant=True, tag=None):
            h = work.tile([P, D, nb * V_BANK, PACK], BF16, name="h")
            for q in range(nb):
                silu_bank(h, q, b, bank0 + q, 1)
            pool(h, b, 0, nb * V_BANK, bank0 * V_BANK, tag)
            if quant:
                quant_z(b, bank0 * V_BANK, nb * V_BANK)
            return h

        def layer2(g0, first, eng, tag=None):
            acc2 = psum2.tile([P, V_HALF], F32, name="acc2")
            for b in range(BLOCKS):
                nc.tensor.matmul_mx(
                    out=acc2[:],
                    lhsT=w2c[:, b * N : (b + 1) * N].bitcast(FP8X4),
                    lhsT_scale=w2s[:, b * N : (b + 1) * N],
                    rhs=zc[b][:, g0 : g0 + V_HALF].bitcast(FP8X4),
                    rhs_scale=zs[b][:, g0 : g0 + V_HALF],
                    start=(b == 0),
                    stop=(b == BLOCKS - 1),
                )
            nv = g0 + V_HALF - first
            if tag:
                y = keep.tile([P, nv], F32, name="y" + tag, tag=tag, align_bytes=64)
            else:
                y = work.tile([P, nv], F32, name="y")
            if eng == "s":
                nc.scalar.copy(y[:], acc2[:, first - g0 :])
            else:
                nc.vector.tensor_copy(y[:], acc2[:, first - g0 :])
            nc.vector.tensor_tensor(
                frame[:].indirect(pos_t[:, first // 16 : (first + nv) // 16]),
                y[:],
                gate_t[:, first : first + nv],
                ALU.mult,
            )

        layer1(0, 0, 4, tag="w1g1")
        w2g = keep.tile([P, BLOCKS, N, PACK], BF16, name="w2g", align_bytes=64)
        for b, copy in enumerate((nc.vector.tensor_copy, nc.vector.tensor_copy)):
            copy(
                w2g[:, b].rearrange("p (c i) j -> p c j i", i=4),
                w2raw[:, b * PACK * N : (b + 1) * PACK * N].rearrange("p (j c i) -> p c j i", j=PACK, i=4),
            )
        w2c = keep.tile([P, BLOCKS * N], U32, name="w2c", align_bytes=64)
        w2s = keep.tile([P, BLOCKS * N], U8, name="w2s", align_bytes=64)
        nc.vector.quantize_mx(
            out=w2c[:].bitcast(FP8X4), scales=w2s[:], in_=w2g[:].rearrange("p b n j -> p (b n j)")
        )
        layer1(0, 4, 3, quant=False)
        quant_z(0, 128, 64)
        layer1(1, 0, 4)
        layer2(0, 0, "s")
        layer1(0, 7, 1, quant=False)
        quant_z(0, 192, 64)
        layer1(1, 4, 2)
        layer1(1, 6, 1, quant=False)
        h = layer1(1, 7, 1, quant=False, tag="last")
        quant_z(1, 192, 64)
        layer2(64, 128, "s", tag="last")
        layer2(128, 192, "s")
        nc.sync.dma_start(out=out, in_=frame[:])
